import numpy as np
import ml_dtypes


def mxq(x, axis, fmt="e4m3"):
    dtype, down = {"e4m3": (ml_dtypes.float8_e4m3fn, 7), "e5m2": (ml_dtypes.float8_e5m2, 14)}[fmt]
    v = np.moveaxis(np.asarray(x, np.float32).astype(ml_dtypes.bfloat16).astype(np.float64), axis, -1)
    blocks = v.reshape(v.shape[:-1] + (-1, 32))
    amax = np.abs(blocks).max(-1, keepdims=True)
    byte = np.maximum(np.where(amax > 0, np.frexp(amax)[1] - 1 + 127, 0) - down, 1)
    scale = np.exp2(byte - 127.0)
    codes = (blocks / scale).astype(np.float32).astype(dtype).astype(np.float64)
    return np.moveaxis((codes * scale).reshape(v.shape), -1, axis)


WIDE = False


def mx_kscale(k):
    if not WIDE:
        return np.ones(k)
    levels = np.array([10, -10, 5, -5, 0])
    if k % 512:
        return np.exp2(np.random.permutation(np.resize(levels, k // 32))).repeat(32)
    a = np.empty((k // 512, 16))
    for p in range(k // 512):
        a[p, :8] = np.random.permutation(np.resize(levels, 8))
        for g in range(8):
            far = levels[np.abs(levels - a[p, g]) >= 10]
            a[p, g + 8] = far[np.random.randint(len(far))]
    return np.exp2(a.ravel()).repeat(32)


def f64(x):
    return np.asarray(x).astype(np.float64)


def striped(idx):
    return np.tile(np.asarray(idx).reshape(-1, 16).T, (8, 1)).astype(np.uint16)


def unstriped(offs):
    return offs[:16].T.reshape(-1).astype(np.int64)


E2M1 = np.array([0.0, 0.5, 1.0, 1.5, 2.0, 3.0, 4.0, 6.0, -0.0, -0.5, -1.0, -1.5, -2.0, -3.0, -4.0, -6.0])


def pack_weight(w, fmt):
    k, n = w.shape
    w = f64(np.asarray(w, np.float32).astype(ml_dtypes.bfloat16)).reshape(k // 32, 32, n)
    amax = np.abs(w).max(1)
    if fmt == "e4m3":
        byte = np.frexp(amax)[1] - 1 + 127 - 7
    else:
        mant, ex = np.frexp(amax / 6.0)
        byte = np.where(mant > 0.5, ex, ex - 1) + 127
    byte = np.clip(np.where(amax > 0, byte, 1), 1, 254)
    scaled = (w * np.exp2(127.0 - byte)[:, None, :]).reshape(k, n).astype(np.float32)
    by_word = np.ascontiguousarray(scaled.reshape(k // 512, 128, 4, n).transpose(0, 1, 3, 2))
    if fmt == "e4m3":
        words = by_word.astype(ml_dtypes.float8_e4m3fn).view(np.uint8)
    else:
        c = by_word.astype(ml_dtypes.float4_e2m1fn).view(np.uint8) & 0xF
        words = (c[..., 0::2] | (c[..., 1::2] << 4)).reshape(k // 512, 128, 2 * n)
    return np.ascontiguousarray(words), np.ascontiguousarray(byte.astype(np.uint8).reshape(k // 512, 16, n))


def unpack_weight(words, scales, fmt):
    g, _, n = scales.shape
    words = np.ascontiguousarray(words).reshape(g, 128, n, -1)
    if fmt == "e4m3":
        vals = words.view(ml_dtypes.float8_e4m3fn).astype(np.float64)
    else:
        nib = np.empty((g, 128, n, 4), np.uint8)
        nib[..., 0::2] = words & 0xF
        nib[..., 1::2] = words >> 4
        vals = E2M1[nib]
    vals = vals * np.repeat(np.exp2(scales.astype(np.float64) - 127.0), 8, axis=1)[..., None]
    return vals.transpose(0, 1, 3, 2).reshape(g * 512, n)


D, T, I, Q, J, U, G, M = 512, 2048, 512, 128, 512, 1024, 64, 512


def setup_inputs():
    n = np.random.standard_normal
    idx = np.random.permutation(T)[:I]
    idx2 = np.random.permutation(U)[:J]
    idx3 = np.random.permutation(M)[:G]
    fd = mx_kscale(D)
    fj = mx_kscale(J)
    tiesp = pack_weight(n((J, T)) * 0.08 / fj[:, None], "e4m3")
    return {
        "query": (n((D, Q)) * 1.0 / np.sqrt(D) * fd[:, None]).astype(np.float32),
        "hubs": (n((D, U)) / fd[:, None]).astype(np.float32),
        "hf": (np.random.uniform(0.5, 2.0, (J, 1)) * fj[:, None]).astype(np.float32),
        "ties_words": tiesp[0],
        "ties_scales": tiesp[1],
        "damp": (np.random.uniform(1.0, 4.0, (Q, 1))).astype(np.float32),
        "worth": np.tile(np.random.uniform(0.2, 2.0, T), (128, 1)).astype(np.float32),
        "old": (1.0 * n((Q, M))).astype(np.float32),
        "offs": striped(idx),
        "offs2": striped(idx2),
        "offs3": striped(idx3),
    }


def reference(query, hubs, hf, ties_words, ties_scales, damp, worth, old, offs, offs2, offs3):
    idx = unstriped(offs)
    idx2 = unstriped(offs2)
    idx3 = unstriped(offs3)
    tiesu = unpack_weight(ties_words, ties_scales, "e4m3")
    hubsidx2q = mxq(f64(hubs)[:, idx2], 0, "e4m3")
    queryq = mxq(f64(query), 0, "e4m3")
    hb = hubsidx2q.T @ queryq
    hp = np.maximum(hb, 0.0) * f64(hf)
    hpq = mxq(hp, 0, "e4m3")
    tiesidxg = tiesu[:, idx]
    s = hpq.T @ tiesidxg
    p = np.exp(s - np.max(s, axis=1, keepdims=True))
    r = p / np.sum(p, axis=1, keepdims=True) * 512.0
    u0 = np.log(r * f64(damp) + 1.0)
    w = u0 / np.sum(u0, axis=1, keepdims=True)
    ws = w * f64(worth)[:1][:, idx] * 512.0
    wp = ws.reshape(Q, G, I // G).sum(axis=2)
    wf = np.zeros((Q, M))
    wf[:, idx3] = wp
    y = f64(old) + wf
    return y

@@ -1,0 +1,212 @@
+from contextlib import ExitStack
+
+import concourse.mybir as mybir
+
+D, T, I, Q, J, U, G, M = 512, 2048, 512, 128, 512, 1024, 64, 512
+FLOPS = 2 * D * J * Q + 2 * J * Q * I
+
+F32 = mybir.dt.float32
+BF16 = mybir.dt.bfloat16
+I32 = mybir.dt.int32
+U32 = mybir.dt.uint32
+U16 = mybir.dt.uint16
+U8 = mybir.dt.uint8
+FP8X4 = mybir.dt.float8_e4m3fn_x4
+ALU = mybir.AluOpType
+ACT = mybir.ActivationFunctionType
+AX = mybir.AxisListType
+
+P = 128
+PACK = 4
+RUN = I // G
+HALF = I // 2
+
+
+def tile_attend_relayed_dampened_pagesums_kernel(
+    tc, query, hubs, hf, ties_words, ties_scales, damp, worth, old, offs, offs2, offs3, out
+):
+    nc = tc.nc
+    with ExitStack() as ctx:
+        sb = ctx.enter_context(tc.tile_pool(name="sb", bufs=1))
+        ps = ctx.enter_context(tc.psum_pool(name="ps", bufs=1))
+
+        hub_list = sb.tile([P, J // 16], U16, name="hub_list")
+        slot_list = sb.tile([P, I // 16], U16, name="slot_list")
+        run_list = sb.tile([P, G // 16], U16, name="run_list")
+        hub_rows = [sb.tile([P, U], F32, name=f"hub_rows{t}") for t in range(PACK)]
+        query_raw = sb.tile([P, PACK, Q], F32, name="query_raw")
+        tie_words = sb.tile([P, T], U32, name="tie_words")
+        tie_bytes = sb.tile([P, T], U8, name="tie_bytes")
+        hub_factor = sb.tile([P, PACK], F32, name="hub_factor")
+        damping = sb.tile([P, 1], F32, name="damping")
+        worth_all = sb.tile([P, T], F32, name="worth_all")
+        old_sums = sb.tile([P, M], F32, name="old_sums")
+        placed = sb.tile([P, M], F32, name="placed")
+
+        nc.vector.memset(tie_bytes[:].bitcast(I32), 0)
+        nc.gpsimd.memset(placed[:], 0.0)
+
+        hubs_by_place = hubs.rearrange("(p t) u -> t p u", t=PACK)
+        nc.sync.dma_start(hub_list[:], offs2)
+        nc.sync.dma_start(hub_rows[0][:], hubs_by_place[0])
+        nc.sync.dma_start(slot_list[:], offs)
+        scale_rows = ties_scales[0].rearrange("(a f) c -> f a c", f=4)
+        for f in range(4):
+            nc.scalar.dma_start(tie_bytes[f:P:32, :].bitcast(I32), scale_rows[f].bitcast(I32))
+        for t in range(1, PACK):
+            nc.sync.dma_start(hub_rows[t][:], hubs_by_place[t])
+        nc.sync.dma_start(query_raw[:], query.rearrange("(p t) q -> p t q", t=PACK))
+        nc.sync.dma_start(
+            tie_words[:].bitcast(I32), ties_words[0].rearrange("p n t -> p (n t)").bitcast(I32)
+        )
+        nc.sync.dma_start(hub_factor[:], hf.rearrange("(p r) o -> p (r o)", r=PACK))
+        nc.sync.dma_start(damping[:], damp)
+        nc.sync.dma_start(worth_all[:], worth)
+        nc.sync.dma_start(run_list[:], offs3)
+        nc.sync.dma_start(old_sums[:], old)
+
+        picked = sb.tile([P, PACK, J], BF16, name="picked")
+
+        def pick_vector(t, a, b):
+            nc.vector.tensor_copy(
+                picked[:, t, a:b], hub_rows[t][:].indirect(hub_list[:, a // 16 : b // 16])
+            )
+
+        def pick_scalar(t, a, b):
+            nc.scalar.activation(
+                picked[:, t, a:b], hub_rows[t][:].indirect(hub_list[:, a // 16 : b // 16]), ACT.Copy
+            )
+
+        slot_words = [sb.tile([P, HALF], U32, name=f"slot_words{h}", align_bytes=64) for h in range(2)]
+        slot_bytes = sb.tile([P, I], U8, name="slot_bytes", align_bytes=64)
+
+        pick_vector(0, 0, J)
+        pick_scalar(1, 0, J)
+        nc.vector.tensor_copy(slot_bytes[:], tie_bytes[:].indirect(slot_list[:]))
+        pick_scalar(2, 0, J)
+        pick_vector(3, 0, J // 2)
+        pick_scalar(3, J // 2, J)
+
+        query_bf = sb.tile([P, Q, PACK], BF16, name="query_bf", align_bytes=64)
+        query_codes = sb.tile([P, Q], U32, name="query_codes", align_bytes=64)
+        query_scales = sb.tile([P, Q], U8, name="query_scales", align_bytes=64)
+        hub_bf = [sb.tile([P, P, PACK], BF16, name=f"hub_bf{r}", align_bytes=64) for r in range(PACK)]
+        hub_codes = [sb.tile([P, P], U32, name=f"hub_codes{r}", align_bytes=64) for r in range(PACK)]
+        hub_scales = [sb.tile([P, P], U8, name=f"hub_scales{r}", align_bytes=64) for r in range(PACK)]
+        dealt = picked[:].rearrange("p t (s r) -> p r s t", r=PACK)
+        hb = ps.tile([P, PACK, Q], F32, name="hb")
+
+        def quantise(codes, scales, values):
+            nc.vector.quantize_mx(
+                out=codes[:].bitcast(FP8X4),
+                scales=scales[:],
+                in_=values[:].rearrange("p c t -> p (c t)"),
+            )
+
+        def hub_product(r):
+            quantise(hub_codes[r], hub_scales[r], hub_bf[r])
+            nc.tensor.matmul_mx(
+                out=hb[:, r, :],
+                lhsT=hub_codes[r][:].bitcast(FP8X4),
+                lhsT_scale=hub_scales[r][:],
+                rhs=query_codes[:].bitcast(FP8X4),
+                rhs_scale=query_scales[:],
+                start=True,
+                stop=True,
+            )
+
+        nc.scalar.copy(query_bf[:], query_raw[:].rearrange("p t q -> p q t"))
+        nc.vector.tensor_copy(hub_bf[0][:], dealt[:, 0])
+        nc.vector.tensor_copy(hub_bf[1][:], dealt[:, 1])
+        nc.scalar.copy(hub_bf[3][:], dealt[:, 3])
+        quantise(query_codes, query_scales, query_bf)
+        hub_product(0)
+        nc.vector.tensor_copy(hub_bf[2][:], dealt[:, 2])
+        hub_product(1)
+        hub_product(3)
+        hub_product(2)
+
+        hp_bf = sb.tile([P, Q, PACK], BF16, name="hp_bf", align_bytes=64)
+        hp_codes = sb.tile([P, Q], U32, name="hp_codes", align_bytes=64)
+        hp_scales = sb.tile([P, Q], U8, name="hp_scales", align_bytes=64)
+        nc.vector.scalar_tensor_tensor(
+            out=hp_bf[:],
+            in0=hb[:].rearrange("p r q -> p q r"),
+            scalar=0.0,
+            in1=hub_factor[:].unsqueeze(1).to_broadcast([P, Q, PACK]),
+            op0=ALU.max,
+            op1=ALU.mult,
+        )
+        half_cols = [slice(h * HALF // 16, (h + 1) * HALF // 16) for h in range(2)]
+        halves = [slice(h * HALF, (h + 1) * HALF) for h in range(2)]
+        nc.vector.tensor_copy(slot_words[0][:], tie_words[:].indirect(slot_list[:, half_cols[0]]))
+        quantise(hp_codes, hp_scales, hp_bf)
+        nc.vector.tensor_copy(slot_words[1][:], tie_words[:].indirect(slot_list[:, half_cols[1]]))
+
+        scores = [ps.tile([P, HALF], F32, name=f"scores{h}") for h in range(2)]
+        neg_max = sb.tile([P, 2], F32, name="neg_max")
+        exp_sums = sb.tile([P, 2], F32, name="exp_sums", tag="after_total")
+        probs = [sb.tile([P, HALF], F32, name=f"probs{h}") for h in range(2)]
+        for h in range(2):
+            nc.tensor.matmul_mx(
+                out=scores[h][:],
+                lhsT=hp_codes[:].bitcast(FP8X4),
+                lhsT_scale=hp_scales[:],
+                rhs=slot_words[h][:].bitcast(FP8X4),
+                rhs_scale=slot_bytes[:, halves[h]],
+                start=True,
+                stop=True,
+            )
+            nc.vector.tensor_reduce(neg_max[:, h : h + 1], scores[h][:], AX.X, ALU.max, negate=True)
+            nc.scalar.activation(
+                probs[h][:], scores[h][:], ACT.Exp, bias=neg_max[:, h : h + 1],
+                accum_out=exp_sums[:, h : h + 1],
+            )
+        neg_row_max = sb.tile([P, 1], F32, name="neg_row_max")
+        nc.vector.tensor_reduce(neg_row_max[:], neg_max[:], AX.X, ALU.min)
+        rebase = sb.tile([P, 2], F32, name="rebase")
+        nc.scalar.activation(rebase[:], neg_max[:], ACT.Exp, bias=neg_row_max[:], scale=-1.0)
+
+        rebased = sb.tile([P, 2], F32, name="rebased")
+        total = sb.tile([P, 1], F32, name="total")
+        nc.vector.scalar_tensor_tensor(
+            out=rebased[:], in0=exp_sums[:], scalar=1.0 / 512.0, in1=rebase[:],
+            op0=ALU.mult, op1=ALU.mult, accum_out=total[:],
+        )
+        worth0 = sb.tile([P, HALF], F32, name="worth0", tag="after_total")
+        nc.vector.tensor_copy(worth0[:], worth_all[:].indirect(slot_list[:, half_cols[0]]))
+        inv_total = sb.tile([P, 1], F32, name="inv_total", tag="after_gain")
+        nc.vector.reciprocal(inv_total[:], total[:])
+        gain = sb.tile([P, 2], F32, name="gain")
+        nc.vector.tensor_scalar(gain[:], rebase[:], inv_total[:], damping[:], ALU.mult, ALU.mult)
+        worth1 = sb.tile([P, HALF], F32, name="worth1", tag="after_gain")
+        nc.vector.tensor_copy(worth1[:], worth_all[:].indirect(slot_list[:, half_cols[1]]))
+        slot_worth = [worth0, worth1]
+
+        parts = [sb.tile([P, HALF], F32, name=f"parts{h}") for h in range(2)]
+        part_sums = sb.tile([P, 2], F32, name="part_sums")
+        weighted = [sb.tile([P, G // 2, RUN], F32, name=f"weighted{h}") for h in range(2)]
+        for h in range(2):
+            nc.scalar.activation(
+                parts[h][:], probs[h][:], ACT.Ln, bias=1.0, scale=gain[:, h : h + 1],
+                accum_out=part_sums[:, h : h + 1],
+            )
+            nc.vector.tensor_tensor(
+                weighted[h][:].rearrange("p g k -> p (g k)"), parts[h][:], slot_worth[h][:], ALU.mult
+            )
+        part_total = sb.tile([P, 1], F32, name="part_total")
+        nc.scalar.activation(part_total[:], part_sums[:, 0:1], ACT.Identity, bias=part_sums[:, 1:2])
+        run_sums = sb.tile([P, G], F32, name="run_sums")
+        inv_parts = sb.tile([P, 1], F32, name="inv_parts")
+        norm = sb.tile([P, G], F32, name="norm")
+        nc.vector.reciprocal(inv_parts[:], part_total[:])
+        nc.vector.tensor_reduce(run_sums[:, 0 : G // 2], weighted[0][:], AX.X, ALU.add)
+        nc.vector.tensor_scalar(norm[:], inv_parts[:].to_broadcast([P, G]), 512.0, None, ALU.mult)
+        nc.vector.tensor_reduce(run_sums[:, G // 2 : G], weighted[1][:], AX.X, ALU.add)
+        nc.vector.tensor_tensor(placed[:].indirect(run_list[:]), run_sums[:], norm[:], ALU.mult)
+
+        for h, queue in enumerate((nc.sync, nc.scalar)):
+            cols = slice(h * M // 2, (h + 1) * M // 2)
+            result = sb.tile([P, M // 2], F32, name=f"result{h}")
+            nc.vector.tensor_tensor(result[:], placed[:, cols], old_sums[:, cols], ALU.add)
+            queue.dma_start(out[:, cols], result[:])

@@ -37,22 +37,25 @@ def tile_attend_relayed_dampened_pagesums_kernel(
         query_raw = sb.tile([P, PACK, Q], F32, name="query_raw")
         tie_words = sb.tile([P, T], U32, name="tie_words")
         tie_bytes = sb.tile([P, T], U8, name="tie_bytes")
-        hub_factor = sb.tile([P, PACK], F32, name="hub_factor")
+        hub_factor = sb.tile([P, PACK], F32, name="hub_factor", tag="after_hp", align_bytes=64)
         damping = sb.tile([P, 1], F32, name="damping")
         worth_all = sb.tile([P, T], F32, name="worth_all")
         old_sums = sb.tile([P, M], F32, name="old_sums")
         placed = sb.tile([P, M], F32, name="placed")
 
         nc.vector.memset(tie_bytes[:].bitcast(I32), 0)
+        nc.gpsimd.dma_start(damping[:], damp)
         nc.gpsimd.memset(placed[:], 0.0)
+        damping512 = sb.tile([P, 1], F32, name="damping512")
+        nc.scalar.activation(damping512[:], damping[:], ACT.Copy, scale=512.0)
 
         hubs_by_place = hubs.rearrange("(p t) u -> t p u", t=PACK)
         nc.sync.dma_start(hub_list[:], offs2)
         nc.sync.dma_start(hub_rows[0][:], hubs_by_place[0])
-        nc.sync.dma_start(slot_list[:], offs)
         scale_rows = ties_scales[0].rearrange("(a f) c -> f a c", f=4)
         for f in range(4):
-            nc.scalar.dma_start(tie_bytes[f:P:32, :].bitcast(I32), scale_rows[f].bitcast(I32))
+            nc.sync.dma_start(tie_bytes[f:P:32, :].bitcast(I32), scale_rows[f].bitcast(I32))
+        nc.sync.dma_start(slot_list[:], offs)
         for t in range(1, PACK):
             nc.sync.dma_start(hub_rows[t][:], hubs_by_place[t])
         nc.sync.dma_start(query_raw[:], query.rearrange("(p t) q -> p t q", t=PACK))
@@ -60,7 +63,6 @@ def tile_attend_relayed_dampened_pagesums_kernel(
             tie_words[:].bitcast(I32), ties_words[0].rearrange("p n t -> p (n t)").bitcast(I32)
         )
         nc.sync.dma_start(hub_factor[:], hf.rearrange("(p r) o -> p (r o)", r=PACK))
-        nc.sync.dma_start(damping[:], damp)
         nc.sync.dma_start(worth_all[:], worth)
         nc.sync.dma_start(run_list[:], offs3)
         nc.sync.dma_start(old_sums[:], old)
@@ -77,7 +79,6 @@ def tile_attend_relayed_dampened_pagesums_kernel(
                 picked[:, t, a:b], hub_rows[t][:].indirect(hub_list[:, a // 16 : b // 16]), ACT.Copy
             )
 
-        slot_words = [sb.tile([P, HALF], U32, name=f"slot_words{h}", align_bytes=64) for h in range(2)]
         slot_bytes = sb.tile([P, I], U8, name="slot_bytes", align_bytes=64)
 
         pick_vector(0, 0, J)
@@ -90,41 +91,44 @@ def tile_attend_relayed_dampened_pagesums_kernel(
         query_bf = sb.tile([P, Q, PACK], BF16, name="query_bf", align_bytes=64)
         query_codes = sb.tile([P, Q], U32, name="query_codes", align_bytes=64)
         query_scales = sb.tile([P, Q], U8, name="query_scales", align_bytes=64)
-        hub_bf = [sb.tile([P, P, PACK], BF16, name=f"hub_bf{r}", align_bytes=64) for r in range(PACK)]
-        hub_codes = [sb.tile([P, P], U32, name=f"hub_codes{r}", align_bytes=64) for r in range(PACK)]
-        hub_scales = [sb.tile([P, P], U8, name=f"hub_scales{r}", align_bytes=64) for r in range(PACK)]
+        hub_codes = sb.tile([P, J], U32, name="hub_codes", align_bytes=64)
+        hub_scales = sb.tile([P, J], U8, name="hub_scales", align_bytes=64)
         dealt = picked[:].rearrange("p t (s r) -> p r s t", r=PACK)
         hb = ps.tile([P, PACK, Q], F32, name="hb")
 
         def quantise(codes, scales, values):
-            nc.vector.quantize_mx(
-                out=codes[:].bitcast(FP8X4),
-                scales=scales[:],
-                in_=values[:].rearrange("p c t -> p (c t)"),
-            )
+            nc.vector.quantize_mx(out=codes.bitcast(FP8X4), scales=scales, in_=values)
 
-        def hub_product(r):
-            quantise(hub_codes[r], hub_scales[r], hub_bf[r])
-            nc.tensor.matmul_mx(
-                out=hb[:, r, :],
-                lhsT=hub_codes[r][:].bitcast(FP8X4),
-                lhsT_scale=hub_scales[r][:],
-                rhs=query_codes[:].bitcast(FP8X4),
-                rhs_scale=query_scales[:],
-                start=True,
-                stop=True,
-            )
+        def hub_products(first, count, values):
+            cols = slice(first * P, (first + count) * P)
+            quantise(hub_codes[:, cols], hub_scales[:, cols], values[:].rearrange("p r s t -> p (r s t)"))
+            for r in range(first, first + count):
+                nc.tensor.matmul_mx(
+                    out=hb[:, r, :],
+                    lhsT=hub_codes[:, r * P : (r + 1) * P].bitcast(FP8X4),
+                    lhsT_scale=hub_scales[:, r * P : (r + 1) * P],
+                    rhs=query_codes[:].bitcast(FP8X4),
+                    rhs_scale=query_scales[:],
+                    start=True,
+                    stop=True,
+                )
 
-        nc.scalar.copy(query_bf[:], query_raw[:].rearrange("p t q -> p q t"))
-        nc.vector.tensor_copy(hub_bf[0][:], dealt[:, 0])
-        nc.vector.tensor_copy(hub_bf[1][:], dealt[:, 1])
-        nc.scalar.copy(hub_bf[3][:], dealt[:, 3])
-        quantise(query_codes, query_scales, query_bf)
-        hub_product(0)
-        nc.vector.tensor_copy(hub_bf[2][:], dealt[:, 2])
-        hub_product(1)
-        hub_product(3)
-        hub_product(2)
+        hub_bf01 = sb.tile([P, 2, P, PACK], BF16, name="hub_bf01", align_bytes=64)
+        hub_bf2 = sb.tile([P, 1, P, PACK], BF16, name="hub_bf2", tag="after_hub2", align_bytes=64)
+        nc.vector.tensor_copy(query_bf[:], query_raw[:].rearrange("p t q -> p q t"))
+        hub_bf3 = sb.tile([P, 1, P, PACK], BF16, name="hub_bf3", align_bytes=64)
+        nc.vector.tensor_copy(hub_bf01[:], dealt[:, 0:2])
+        nc.scalar.copy(hub_bf2[:], dealt[:, 2:3])
+        nc.scalar.copy(hub_bf3[:], dealt[:, 3:4])
+        quantise(query_codes[:], query_scales[:], query_bf[:].rearrange("p q t -> p (q t)"))
+        hub_products(0, 2, hub_bf01)
+        hub_products(2, 1, hub_bf2)
+        hub_products(3, 1, hub_bf3)
+
+        half_cols = [slice(h * HALF // 16, (h + 1) * HALF // 16) for h in range(2)]
+        halves = [slice(h * HALF, (h + 1) * HALF) for h in range(2)]
+        slot_words0 = sb.tile([P, HALF], U32, name="slot_words0", tag="after_hub2", align_bytes=64)
+        nc.vector.tensor_copy(slot_words0[:], tie_words[:].indirect(slot_list[:, half_cols[0]]))
 
         hp_bf = sb.tile([P, Q, PACK], BF16, name="hp_bf", align_bytes=64)
         hp_codes = sb.tile([P, Q], U32, name="hp_codes", align_bytes=64)
@@ -137,16 +141,15 @@ def tile_attend_relayed_dampened_pagesums_kernel(
             op0=ALU.max,
             op1=ALU.mult,
         )
-        half_cols = [slice(h * HALF // 16, (h + 1) * HALF // 16) for h in range(2)]
-        halves = [slice(h * HALF, (h + 1) * HALF) for h in range(2)]
-        nc.vector.tensor_copy(slot_words[0][:], tie_words[:].indirect(slot_list[:, half_cols[0]]))
-        quantise(hp_codes, hp_scales, hp_bf)
-        nc.vector.tensor_copy(slot_words[1][:], tie_words[:].indirect(slot_list[:, half_cols[1]]))
+        quantise(hp_codes[:], hp_scales[:], hp_bf[:].rearrange("p q r -> p (q r)"))
+        slot_words1 = sb.tile([P, HALF], U32, name="slot_words1", tag="after_hp", align_bytes=64)
+        nc.vector.tensor_copy(slot_words1[:], tie_words[:].indirect(slot_list[:, half_cols[1]]))
+        slot_words = [slot_words0, slot_words1]
 
         scores = [ps.tile([P, HALF], F32, name=f"scores{h}") for h in range(2)]
         neg_max = sb.tile([P, 2], F32, name="neg_max")
-        exp_sums = sb.tile([P, 2], F32, name="exp_sums", tag="after_total")
-        probs = [sb.tile([P, HALF], F32, name=f"probs{h}") for h in range(2)]
+        exp_sums = sb.tile([P, 2], F32, name="exp_sums")
+        probs = [sb.tile([P, HALF], F32, name=f"probs{h}", tag=f"probs{h}") for h in range(2)]
         for h in range(2):
             nc.tensor.matmul_mx(
                 out=scores[h][:],
@@ -162,24 +165,24 @@ def tile_attend_relayed_dampened_pagesums_kernel(
                 probs[h][:], scores[h][:], ACT.Exp, bias=neg_max[:, h : h + 1],
                 accum_out=exp_sums[:, h : h + 1],
             )
-        neg_row_max = sb.tile([P, 1], F32, name="neg_row_max")
+        neg_row_max = sb.tile([P, 1], F32, name="neg_row_max", tag="after_rebase")
         nc.vector.tensor_reduce(neg_row_max[:], neg_max[:], AX.X, ALU.min)
         rebase = sb.tile([P, 2], F32, name="rebase")
         nc.scalar.activation(rebase[:], neg_max[:], ACT.Exp, bias=neg_row_max[:], scale=-1.0)
 
         rebased = sb.tile([P, 2], F32, name="rebased")
-        total = sb.tile([P, 1], F32, name="total")
+        total = sb.tile([P, 1], F32, name="total", tag="after_inverse")
         nc.vector.scalar_tensor_tensor(
-            out=rebased[:], in0=exp_sums[:], scalar=1.0 / 512.0, in1=rebase[:],
+            out=rebased[:], in0=exp_sums[:], scalar=1.0, in1=rebase[:],
             op0=ALU.mult, op1=ALU.mult, accum_out=total[:],
         )
-        worth0 = sb.tile([P, HALF], F32, name="worth0", tag="after_total")
+        worth0 = sb.tile([P, HALF], F32, name="worth0", tag="after_rebase")
         nc.vector.tensor_copy(worth0[:], worth_all[:].indirect(slot_list[:, half_cols[0]]))
-        inv_total = sb.tile([P, 1], F32, name="inv_total", tag="after_gain")
+        inv_total = sb.tile([P, 1], F32, name="inv_total")
         nc.vector.reciprocal(inv_total[:], total[:])
         gain = sb.tile([P, 2], F32, name="gain")
-        nc.vector.tensor_scalar(gain[:], rebase[:], inv_total[:], damping[:], ALU.mult, ALU.mult)
-        worth1 = sb.tile([P, HALF], F32, name="worth1", tag="after_gain")
+        nc.vector.tensor_scalar(gain[:], rebase[:], inv_total[:], damping512[:], ALU.mult, ALU.mult)
+        worth1 = sb.tile([P, HALF], F32, name="worth1", tag="after_inverse")
         nc.vector.tensor_copy(worth1[:], worth_all[:].indirect(slot_list[:, half_cols[1]]))
         slot_worth = [worth0, worth1]
 
@@ -196,12 +199,12 @@ def tile_attend_relayed_dampened_pagesums_kernel(
             )
         part_total = sb.tile([P, 1], F32, name="part_total")
         nc.scalar.activation(part_total[:], part_sums[:, 0:1], ACT.Identity, bias=part_sums[:, 1:2])
-        run_sums = sb.tile([P, G], F32, name="run_sums")
+        run_sums = sb.tile([P, G], F32, name="run_sums", tag="probs1")
         inv_parts = sb.tile([P, 1], F32, name="inv_parts")
         norm = sb.tile([P, G], F32, name="norm")
         nc.vector.reciprocal(inv_parts[:], part_total[:])
         nc.vector.tensor_reduce(run_sums[:, 0 : G // 2], weighted[0][:], AX.X, ALU.add)
-        nc.vector.tensor_scalar(norm[:], inv_parts[:].to_broadcast([P, G]), 512.0, None, ALU.mult)
+        nc.scalar.activation(norm[:], inv_parts[:].to_broadcast([P, G]), ACT.Copy, scale=512.0)
         nc.vector.tensor_reduce(run_sums[:, G // 2 : G], weighted[1][:], AX.X, ALU.add)
         nc.vector.tensor_tensor(placed[:].indirect(run_list[:]), run_sums[:], norm[:], ALU.mult)
 

@@ -44,8 +44,8 @@ def tile_attend_relayed_dampened_pagesums_kernel(
         placed = sb.tile([P, M], F32, name="placed")
 
         nc.vector.memset(tie_bytes[:].bitcast(I32), 0)
-        nc.gpsimd.dma_start(damping[:], damp)
-        nc.gpsimd.memset(placed[:], 0.0)
+        nc.scalar.dma_start(damping[:], damp)
+        nc.vector.memset(placed[:], 0.0)
         damping512 = sb.tile([P, 1], F32, name="damping512")
         nc.scalar.activation(damping512[:], damping[:], ACT.Copy, scale=512.0)
 
@@ -55,8 +55,9 @@ def tile_attend_relayed_dampened_pagesums_kernel(
         scale_rows = ties_scales[0].rearrange("(a f) c -> f a c", f=4)
         for f in range(4):
             nc.sync.dma_start(tie_bytes[f:P:32, :].bitcast(I32), scale_rows[f].bitcast(I32))
+        nc.sync.dma_start(hub_rows[1][:], hubs_by_place[1])
         nc.sync.dma_start(slot_list[:], offs)
-        for t in range(1, PACK):
+        for t in range(2, PACK):
             nc.sync.dma_start(hub_rows[t][:], hubs_by_place[t])
         nc.sync.dma_start(query_raw[:], query.rearrange("(p t) q -> p t q", t=PACK))
         nc.sync.dma_start(

@@ -18,8 +18,11 @@ AX = mybir.AxisListType
 
 P = 128
 PACK = 4
+PER_COLUMN = 16
 RUN = I // G
 HALF = I // 2
+GAIN = 512.0
+SCALE_STEP = 8
 
 
 def tile_attend_relayed_dampened_pagesums_kernel(
@@ -30,64 +33,68 @@ def tile_attend_relayed_dampened_pagesums_kernel(
         sb = ctx.enter_context(tc.tile_pool(name="sb", bufs=1))
         ps = ctx.enter_context(tc.psum_pool(name="ps", bufs=1))
 
-        hub_list = sb.tile([P, J // 16], U16, name="hub_list")
-        slot_list = sb.tile([P, I // 16], U16, name="slot_list")
-        run_list = sb.tile([P, G // 16], U16, name="run_list")
-        hub_rows = [sb.tile([P, U], F32, name=f"hub_rows{t}") for t in range(PACK)]
+        hub_list = sb.tile([P, J // PER_COLUMN], U16, name="hub_list")
+        slot_list = sb.tile([P, I // PER_COLUMN], U16, name="slot_list")
+        run_list = sb.tile([P, G // PER_COLUMN], U16, name="run_list")
+        hub_rows = [sb.tile([P, U], F32, name=f"hub_rows{t}", tag=f"hub_rows{t}") for t in range(PACK)]
         query_raw = sb.tile([P, PACK, Q], F32, name="query_raw")
         tie_words = sb.tile([P, T], U32, name="tie_words")
         tie_bytes = sb.tile([P, T], U8, name="tie_bytes")
         hub_factor = sb.tile([P, PACK], F32, name="hub_factor", tag="after_hp", align_bytes=64)
         damping = sb.tile([P, 1], F32, name="damping")
-        worth_all = sb.tile([P, T], F32, name="worth_all")
-        old_sums = sb.tile([P, M], F32, name="old_sums")
         placed = sb.tile([P, M], F32, name="placed")
 
         nc.vector.memset(tie_bytes[:].bitcast(I32), 0)
         nc.scalar.dma_start(damping[:], damp)
         nc.vector.memset(placed[:], 0.0)
-        damping512 = sb.tile([P, 1], F32, name="damping512")
-        nc.scalar.activation(damping512[:], damping[:], ACT.Copy, scale=512.0)
+        damping_gain = sb.tile([P, 1], F32, name="damping_gain")
+        nc.scalar.activation(damping_gain[:], damping[:], ACT.Copy, scale=GAIN)
 
         hubs_by_place = hubs.rearrange("(p t) u -> t p u", t=PACK)
-        nc.sync.dma_start(hub_list[:], offs2)
         nc.sync.dma_start(hub_rows[0][:], hubs_by_place[0])
-        scale_rows = ties_scales[0].rearrange("(a f) c -> f a c", f=4)
-        for f in range(4):
-            nc.sync.dma_start(tie_bytes[f:P:32, :].bitcast(I32), scale_rows[f].bitcast(I32))
-        nc.sync.dma_start(hub_rows[1][:], hubs_by_place[1])
+        nc.sync.dma_start(hub_list[:], offs2)
         nc.sync.dma_start(slot_list[:], offs)
-        for t in range(2, PACK):
+        nc.sync.dma_start(tie_bytes[0:P:SCALE_STEP, :].bitcast(I32), ties_scales[0].bitcast(I32))
+        for t in range(1, PACK):
             nc.sync.dma_start(hub_rows[t][:], hubs_by_place[t])
         nc.sync.dma_start(query_raw[:], query.rearrange("(p t) q -> p t q", t=PACK))
         nc.sync.dma_start(
             tie_words[:].bitcast(I32), ties_words[0].rearrange("p n t -> p (n t)").bitcast(I32)
         )
         nc.sync.dma_start(hub_factor[:], hf.rearrange("(p r) o -> p (r o)", r=PACK))
-        nc.sync.dma_start(worth_all[:], worth)
         nc.sync.dma_start(run_list[:], offs3)
-        nc.sync.dma_start(old_sums[:], old)
 
         picked = sb.tile([P, PACK, J], BF16, name="picked")
 
-        def pick_vector(t, a, b):
-            nc.vector.tensor_copy(
-                picked[:, t, a:b], hub_rows[t][:].indirect(hub_list[:, a // 16 : b // 16])
-            )
+        def listed_hubs(t, first, last):
+            return hub_rows[t][:].indirect(hub_list[:, first // PER_COLUMN : last // PER_COLUMN])
 
-        def pick_scalar(t, a, b):
-            nc.scalar.activation(
-                picked[:, t, a:b], hub_rows[t][:].indirect(hub_list[:, a // 16 : b // 16]), ACT.Copy
-            )
+        def pick_on_vector(t, first, last):
+            nc.vector.tensor_copy(picked[:, t, first:last], listed_hubs(t, first, last))
+
+        def pick_on_scalar(t, first, last):
+            nc.scalar.activation(picked[:, t, first:last], listed_hubs(t, first, last), ACT.Copy)
 
         slot_bytes = sb.tile([P, I], U8, name="slot_bytes", align_bytes=64)
 
-        pick_vector(0, 0, J)
-        pick_scalar(1, 0, J)
+        pick_on_vector(0, 0, J)
+        pick_on_scalar(1, 0, J)
         nc.vector.tensor_copy(slot_bytes[:], tie_bytes[:].indirect(slot_list[:]))
-        pick_scalar(2, 0, J)
-        pick_vector(3, 0, J // 2)
-        pick_scalar(3, J // 2, J)
+        slot_scales = sb.tile([P, I], U8, name="slot_scales", align_bytes=64)
+        nc.vector.tensor_copy(slot_scales[:].bitcast(I32), slot_bytes[:].bitcast(I32))
+        for f in range(1, 4):
+            nc.sync.dma_start(
+                slot_scales[f:P:32, :].bitcast(I32),
+                slot_bytes[SCALE_STEP * f : P : 32, :].bitcast(I32),
+            )
+        pick_on_vector(2, 0, J // 2)
+        pick_on_scalar(2, J // 2, J)
+        pick_on_vector(3, 0, J // 2)
+        pick_on_scalar(3, J // 2, J)
+        worth_all = sb.tile([P, T], F32, name="worth_all", tag="hub_rows2")
+        old_sums = sb.tile([P, M], F32, name="old_sums", tag="hub_rows3")
+        nc.sync.dma_start(worth_all[:], worth)
+        nc.sync.dma_start(old_sums[:], old)
 
         query_bf = sb.tile([P, Q, PACK], BF16, name="query_bf", align_bytes=64)
         query_codes = sb.tile([P, Q], U32, name="query_codes", align_bytes=64)
@@ -100,10 +107,12 @@ def tile_attend_relayed_dampened_pagesums_kernel(
         def quantise(codes, scales, values):
             nc.vector.quantize_mx(out=codes.bitcast(FP8X4), scales=scales, in_=values)
 
-        def hub_products(first, count, values):
-            cols = slice(first * P, (first + count) * P)
+        def quantise_hubs(first_r, count, values):
+            cols = slice(first_r * P, (first_r + count) * P)
             quantise(hub_codes[:, cols], hub_scales[:, cols], values[:].rearrange("p r s t -> p (r s t)"))
-            for r in range(first, first + count):
+
+        def hub_products(first_r, count):
+            for r in range(first_r, first_r + count):
                 nc.tensor.matmul_mx(
                     out=hb[:, r, :],
                     lhsT=hub_codes[:, r * P : (r + 1) * P].bitcast(FP8X4),
@@ -121,15 +130,18 @@ def tile_attend_relayed_dampened_pagesums_kernel(
         nc.vector.tensor_copy(hub_bf01[:], dealt[:, 0:2])
         nc.scalar.copy(hub_bf2[:], dealt[:, 2:3])
         nc.scalar.copy(hub_bf3[:], dealt[:, 3:4])
+        quantise_hubs(0, 2, hub_bf01)
         quantise(query_codes[:], query_scales[:], query_bf[:].rearrange("p q t -> p (q t)"))
-        hub_products(0, 2, hub_bf01)
-        hub_products(2, 1, hub_bf2)
-        hub_products(3, 1, hub_bf3)
+        hub_products(0, 2)
+        quantise_hubs(2, 1, hub_bf2)
+        hub_products(2, 1)
+        quantise_hubs(3, 1, hub_bf3)
+        hub_products(3, 1)
 
-        half_cols = [slice(h * HALF // 16, (h + 1) * HALF // 16) for h in range(2)]
-        halves = [slice(h * HALF, (h + 1) * HALF) for h in range(2)]
+        list_halves = [slice(h * HALF // PER_COLUMN, (h + 1) * HALF // PER_COLUMN) for h in range(2)]
+        slot_halves = [slice(h * HALF, (h + 1) * HALF) for h in range(2)]
         slot_words0 = sb.tile([P, HALF], U32, name="slot_words0", tag="after_hub2", align_bytes=64)
-        nc.vector.tensor_copy(slot_words0[:], tie_words[:].indirect(slot_list[:, half_cols[0]]))
+        nc.vector.tensor_copy(slot_words0[:], tie_words[:].indirect(slot_list[:, list_halves[0]]))
 
         hp_bf = sb.tile([P, Q, PACK], BF16, name="hp_bf", align_bytes=64)
         hp_codes = sb.tile([P, Q], U32, name="hp_codes", align_bytes=64)
@@ -144,26 +156,29 @@ def tile_attend_relayed_dampened_pagesums_kernel(
         )
         quantise(hp_codes[:], hp_scales[:], hp_bf[:].rearrange("p q r -> p (q r)"))
         slot_words1 = sb.tile([P, HALF], U32, name="slot_words1", tag="after_hp", align_bytes=64)
-        nc.vector.tensor_copy(slot_words1[:], tie_words[:].indirect(slot_list[:, half_cols[1]]))
+        nc.vector.tensor_copy(slot_words1[:], tie_words[:].indirect(slot_list[:, list_halves[1]]))
         slot_words = [slot_words0, slot_words1]
 
         scores = [ps.tile([P, HALF], F32, name=f"scores{h}") for h in range(2)]
         neg_max = sb.tile([P, 2], F32, name="neg_max")
         exp_sums = sb.tile([P, 2], F32, name="exp_sums")
-        probs = [sb.tile([P, HALF], F32, name=f"probs{h}", tag=f"probs{h}") for h in range(2)]
+        probs = [sb.tile([P, HALF], F32, name=f"probs{h}") for h in range(2)]
         for h in range(2):
             nc.tensor.matmul_mx(
                 out=scores[h][:],
                 lhsT=hp_codes[:].bitcast(FP8X4),
                 lhsT_scale=hp_scales[:],
                 rhs=slot_words[h][:].bitcast(FP8X4),
-                rhs_scale=slot_bytes[:, halves[h]],
+                rhs_scale=slot_scales[:, slot_halves[h]],
                 start=True,
                 stop=True,
             )
             nc.vector.tensor_reduce(neg_max[:, h : h + 1], scores[h][:], AX.X, ALU.max, negate=True)
             nc.scalar.activation(
-                probs[h][:], scores[h][:], ACT.Exp, bias=neg_max[:, h : h + 1],
+                probs[h][:],
+                scores[h][:],
+                ACT.Exp,
+                bias=neg_max[:, h : h + 1],
                 accum_out=exp_sums[:, h : h + 1],
             )
         neg_row_max = sb.tile([P, 1], F32, name="neg_row_max", tag="after_rebase")
@@ -174,25 +189,34 @@ def tile_attend_relayed_dampened_pagesums_kernel(
         rebased = sb.tile([P, 2], F32, name="rebased")
         total = sb.tile([P, 1], F32, name="total", tag="after_inverse")
         nc.vector.scalar_tensor_tensor(
-            out=rebased[:], in0=exp_sums[:], scalar=1.0, in1=rebase[:],
-            op0=ALU.mult, op1=ALU.mult, accum_out=total[:],
+            out=rebased[:],
+            in0=exp_sums[:],
+            scalar=1.0,
+            in1=rebase[:],
+            op0=ALU.mult,
+            op1=ALU.mult,
+            accum_out=total[:],
         )
         worth0 = sb.tile([P, HALF], F32, name="worth0", tag="after_rebase")
-        nc.vector.tensor_copy(worth0[:], worth_all[:].indirect(slot_list[:, half_cols[0]]))
+        nc.vector.tensor_copy(worth0[:], worth_all[:].indirect(slot_list[:, list_halves[0]]))
         inv_total = sb.tile([P, 1], F32, name="inv_total")
         nc.vector.reciprocal(inv_total[:], total[:])
-        gain = sb.tile([P, 2], F32, name="gain")
-        nc.vector.tensor_scalar(gain[:], rebase[:], inv_total[:], damping512[:], ALU.mult, ALU.mult)
+        ln_scale = sb.tile([P, 2], F32, name="ln_scale")
+        nc.vector.tensor_scalar(ln_scale[:], rebase[:], inv_total[:], damping_gain[:], ALU.mult, ALU.mult)
         worth1 = sb.tile([P, HALF], F32, name="worth1", tag="after_inverse")
-        nc.vector.tensor_copy(worth1[:], worth_all[:].indirect(slot_list[:, half_cols[1]]))
+        nc.vector.tensor_copy(worth1[:], worth_all[:].indirect(slot_list[:, list_halves[1]]))
         slot_worth = [worth0, worth1]
 
         parts = [sb.tile([P, HALF], F32, name=f"parts{h}") for h in range(2)]
-        part_sums = sb.tile([P, 2], F32, name="part_sums")
+        part_sums = sb.tile([P, 2], F32, name="part_sums", tag="after_part_total")
         weighted = [sb.tile([P, G // 2, RUN], F32, name=f"weighted{h}") for h in range(2)]
         for h in range(2):
             nc.scalar.activation(
-                parts[h][:], probs[h][:], ACT.Ln, bias=1.0, scale=gain[:, h : h + 1],
+                parts[h][:],
+                probs[h][:],
+                ACT.Ln,
+                bias=1.0,
+                scale=ln_scale[:, h : h + 1],
                 accum_out=part_sums[:, h : h + 1],
             )
             nc.vector.tensor_tensor(
@@ -200,12 +224,12 @@ def tile_attend_relayed_dampened_pagesums_kernel(
             )
         part_total = sb.tile([P, 1], F32, name="part_total")
         nc.scalar.activation(part_total[:], part_sums[:, 0:1], ACT.Identity, bias=part_sums[:, 1:2])
-        run_sums = sb.tile([P, G], F32, name="run_sums", tag="probs1")
+        run_sums = sb.tile([P, G], F32, name="run_sums", tag="after_part_total")
         inv_parts = sb.tile([P, 1], F32, name="inv_parts")
         norm = sb.tile([P, G], F32, name="norm")
         nc.vector.reciprocal(inv_parts[:], part_total[:])
         nc.vector.tensor_reduce(run_sums[:, 0 : G // 2], weighted[0][:], AX.X, ALU.add)
-        nc.scalar.activation(norm[:], inv_parts[:].to_broadcast([P, G]), ACT.Copy, scale=512.0)
+        nc.vector.tensor_scalar(norm[:], inv_parts[:].to_broadcast([P, G]), GAIN, None, ALU.mult)
         nc.vector.tensor_reduce(run_sums[:, G // 2 : G], weighted[1][:], AX.X, ALU.add)
         nc.vector.tensor_tensor(placed[:].indirect(run_list[:]), run_sums[:], norm[:], ALU.mult)
 

from contextlib import ExitStack

import concourse.mybir as mybir

D, T, I, Q, J, U, G, M = 512, 2048, 512, 128, 512, 1024, 64, 512
FLOPS = 2 * D * J * Q + 2 * J * Q * I

F32 = mybir.dt.float32
BF16 = mybir.dt.bfloat16
I32 = mybir.dt.int32
U32 = mybir.dt.uint32
U16 = mybir.dt.uint16
U8 = mybir.dt.uint8
FP8X4 = mybir.dt.float8_e4m3fn_x4
ALU = mybir.AluOpType
ACT = mybir.ActivationFunctionType
AX = mybir.AxisListType

P = 128
PACK = 4
PER_COLUMN = 16
RUN = I // G
HALF = I // 2
GAIN = 512.0
SCALE_STEP = 8


def tile_attend_relayed_dampened_pagesums_kernel(
    tc, query, hubs, hf, ties_words, ties_scales, damp, worth, old, offs, offs2, offs3, out
):
    nc = tc.nc
    with ExitStack() as ctx:
        sb = ctx.enter_context(tc.tile_pool(name="sb", bufs=1))
        ps = ctx.enter_context(tc.psum_pool(name="ps", bufs=1))

        hub_list = sb.tile([P, J // PER_COLUMN], U16, name="hub_list")
        slot_list = sb.tile([P, I // PER_COLUMN], U16, name="slot_list")
        run_list = sb.tile([P, G // PER_COLUMN], U16, name="run_list")
        hub_rows = [sb.tile([P, U], F32, name=f"hub_rows{t}", tag=f"hub_rows{t}") for t in range(PACK)]
        query_raw = sb.tile([P, PACK, Q], F32, name="query_raw")
        tie_words = sb.tile([P, T], U32, name="tie_words")
        tie_bytes = sb.tile([P, T], U8, name="tie_bytes")
        hub_factor = sb.tile([P, PACK], F32, name="hub_factor", tag="after_hp", align_bytes=64)
        damping = sb.tile([P, 1], F32, name="damping")
        placed = sb.tile([P, M], F32, name="placed")

        nc.vector.memset(tie_bytes[:].bitcast(I32), 0)
        nc.scalar.dma_start(damping[:], damp)
        nc.vector.memset(placed[:], 0.0)
        damping_gain = sb.tile([P, 1], F32, name="damping_gain")
        nc.scalar.activation(damping_gain[:], damping[:], ACT.Copy, scale=GAIN)

        hubs_by_place = hubs.rearrange("(p t) u -> t p u", t=PACK)
        nc.sync.dma_start(hub_rows[0][:], hubs_by_place[0])
        nc.sync.dma_start(hub_list[:], offs2)
        nc.sync.dma_start(slot_list[:], offs)
        nc.sync.dma_start(tie_bytes[0:P:SCALE_STEP, :].bitcast(I32), ties_scales[0].bitcast(I32))
        for t in range(1, PACK):
            nc.sync.dma_start(hub_rows[t][:], hubs_by_place[t])
        nc.sync.dma_start(query_raw[:], query.rearrange("(p t) q -> p t q", t=PACK))
        nc.sync.dma_start(
            tie_words[:].bitcast(I32), ties_words[0].rearrange("p n t -> p (n t)").bitcast(I32)
        )
        nc.sync.dma_start(hub_factor[:], hf.rearrange("(p r) o -> p (r o)", r=PACK))
        nc.sync.dma_start(run_list[:], offs3)

        picked = sb.tile([P, PACK, J], BF16, name="picked")

        def listed_hubs(t, first, last):
            return hub_rows[t][:].indirect(hub_list[:, first // PER_COLUMN : last // PER_COLUMN])

        def pick_on_vector(t, first, last):
            nc.vector.tensor_copy(picked[:, t, first:last], listed_hubs(t, first, last))

        def pick_on_scalar(t, first, last):
            nc.scalar.activation(picked[:, t, first:last], listed_hubs(t, first, last), ACT.Copy)

        slot_bytes = sb.tile([P, I], U8, name="slot_bytes", align_bytes=64)

        pick_on_vector(0, 0, J)
        pick_on_scalar(1, 0, J)
        nc.vector.tensor_copy(slot_bytes[:], tie_bytes[:].indirect(slot_list[:]))
        slot_scales = sb.tile([P, I], U8, name="slot_scales", align_bytes=64)
        nc.vector.tensor_copy(slot_scales[:].bitcast(I32), slot_bytes[:].bitcast(I32))
        for f in range(1, 4):
            nc.sync.dma_start(
                slot_scales[f:P:32, :].bitcast(I32),
                slot_bytes[SCALE_STEP * f : P : 32, :].bitcast(I32),
            )
        pick_on_vector(2, 0, J // 2)
        pick_on_scalar(2, J // 2, J)
        pick_on_vector(3, 0, J // 2)
        pick_on_scalar(3, J // 2, J)
        worth_all = sb.tile([P, T], F32, name="worth_all", tag="hub_rows2")
        old_sums = sb.tile([P, M], F32, name="old_sums", tag="hub_rows3")
        nc.sync.dma_start(worth_all[:], worth)
        nc.sync.dma_start(old_sums[:], old)

        query_bf = sb.tile([P, Q, PACK], BF16, name="query_bf", align_bytes=64)
        query_codes = sb.tile([P, Q], U32, name="query_codes", align_bytes=64)
        query_scales = sb.tile([P, Q], U8, name="query_scales", align_bytes=64)
        hub_codes = sb.tile([P, J], U32, name="hub_codes", align_bytes=64)
        hub_scales = sb.tile([P, J], U8, name="hub_scales", align_bytes=64)
        dealt = picked[:].rearrange("p t (s r) -> p r s t", r=PACK)
        hb = ps.tile([P, PACK, Q], F32, name="hb")

        def quantise(codes, scales, values):
            nc.vector.quantize_mx(out=codes.bitcast(FP8X4), scales=scales, in_=values)

        def quantise_hubs(first_r, count, values):
            cols = slice(first_r * P, (first_r + count) * P)
            quantise(hub_codes[:, cols], hub_scales[:, cols], values[:].rearrange("p r s t -> p (r s t)"))

        def hub_products(first_r, count):
            for r in range(first_r, first_r + count):
                nc.tensor.matmul_mx(
                    out=hb[:, r, :],
                    lhsT=hub_codes[:, r * P : (r + 1) * P].bitcast(FP8X4),
                    lhsT_scale=hub_scales[:, r * P : (r + 1) * P],
                    rhs=query_codes[:].bitcast(FP8X4),
                    rhs_scale=query_scales[:],
                    start=True,
                    stop=True,
                )

        hub_bf01 = sb.tile([P, 2, P, PACK], BF16, name="hub_bf01", align_bytes=64)
        hub_bf2 = sb.tile([P, 1, P, PACK], BF16, name="hub_bf2", tag="after_hub2", align_bytes=64)
        nc.vector.tensor_copy(query_bf[:], query_raw[:].rearrange("p t q -> p q t"))
        hub_bf3 = sb.tile([P, 1, P, PACK], BF16, name="hub_bf3", align_bytes=64)
        nc.vector.tensor_copy(hub_bf01[:], dealt[:, 0:2])
        nc.scalar.copy(hub_bf2[:], dealt[:, 2:3])
        nc.scalar.copy(hub_bf3[:], dealt[:, 3:4])
        quantise_hubs(0, 2, hub_bf01)
        quantise(query_codes[:], query_scales[:], query_bf[:].rearrange("p q t -> p (q t)"))
        hub_products(0, 2)
        quantise_hubs(2, 1, hub_bf2)
        hub_products(2, 1)
        quantise_hubs(3, 1, hub_bf3)
        hub_products(3, 1)

        list_halves = [slice(h * HALF // PER_COLUMN, (h + 1) * HALF // PER_COLUMN) for h in range(2)]
        slot_halves = [slice(h * HALF, (h + 1) * HALF) for h in range(2)]
        slot_words0 = sb.tile([P, HALF], U32, name="slot_words0", tag="after_hub2", align_bytes=64)
        nc.vector.tensor_copy(slot_words0[:], tie_words[:].indirect(slot_list[:, list_halves[0]]))

        hp_bf = sb.tile([P, Q, PACK], BF16, name="hp_bf", align_bytes=64)
        hp_codes = sb.tile([P, Q], U32, name="hp_codes", align_bytes=64)
        hp_scales = sb.tile([P, Q], U8, name="hp_scales", align_bytes=64)
        nc.vector.scalar_tensor_tensor(
            out=hp_bf[:],
            in0=hb[:].rearrange("p r q -> p q r"),
            scalar=0.0,
            in1=hub_factor[:].unsqueeze(1).to_broadcast([P, Q, PACK]),
            op0=ALU.max,
            op1=ALU.mult,
        )
        quantise(hp_codes[:], hp_scales[:], hp_bf[:].rearrange("p q r -> p (q r)"))
        slot_words1 = sb.tile([P, HALF], U32, name="slot_words1", tag="after_hp", align_bytes=64)
        nc.vector.tensor_copy(slot_words1[:], tie_words[:].indirect(slot_list[:, list_halves[1]]))
        slot_words = [slot_words0, slot_words1]

        scores = [ps.tile([P, HALF], F32, name=f"scores{h}") for h in range(2)]
        neg_max = sb.tile([P, 2], F32, name="neg_max")
        exp_sums = sb.tile([P, 2], F32, name="exp_sums")
        probs = [sb.tile([P, HALF], F32, name=f"probs{h}") for h in range(2)]
        for h in range(2):
            nc.tensor.matmul_mx(
                out=scores[h][:],
                lhsT=hp_codes[:].bitcast(FP8X4),
                lhsT_scale=hp_scales[:],
                rhs=slot_words[h][:].bitcast(FP8X4),
                rhs_scale=slot_scales[:, slot_halves[h]],
                start=True,
                stop=True,
            )
            nc.vector.tensor_reduce(neg_max[:, h : h + 1], scores[h][:], AX.X, ALU.max, negate=True)
            nc.scalar.activation(
                probs[h][:],
                scores[h][:],
                ACT.Exp,
                bias=neg_max[:, h : h + 1],
                accum_out=exp_sums[:, h : h + 1],
            )
        neg_row_max = sb.tile([P, 1], F32, name="neg_row_max", tag="after_rebase")
        nc.vector.tensor_reduce(neg_row_max[:], neg_max[:], AX.X, ALU.min)
        rebase = sb.tile([P, 2], F32, name="rebase")
        nc.scalar.activation(rebase[:], neg_max[:], ACT.Exp, bias=neg_row_max[:], scale=-1.0)

        rebased = sb.tile([P, 2], F32, name="rebased")
        total = sb.tile([P, 1], F32, name="total", tag="after_inverse")
        nc.vector.scalar_tensor_tensor(
            out=rebased[:],
            in0=exp_sums[:],
            scalar=1.0,
            in1=rebase[:],
            op0=ALU.mult,
            op1=ALU.mult,
            accum_out=total[:],
        )
        worth0 = sb.tile([P, HALF], F32, name="worth0", tag="after_rebase")
        nc.vector.tensor_copy(worth0[:], worth_all[:].indirect(slot_list[:, list_halves[0]]))
        inv_total = sb.tile([P, 1], F32, name="inv_total")
        nc.vector.reciprocal(inv_total[:], total[:])
        ln_scale = sb.tile([P, 2], F32, name="ln_scale")
        nc.vector.tensor_scalar(ln_scale[:], rebase[:], inv_total[:], damping_gain[:], ALU.mult, ALU.mult)
        worth1 = sb.tile([P, HALF], F32, name="worth1", tag="after_inverse")
        nc.vector.tensor_copy(worth1[:], worth_all[:].indirect(slot_list[:, list_halves[1]]))
        slot_worth = [worth0, worth1]

        parts = [sb.tile([P, HALF], F32, name=f"parts{h}") for h in range(2)]
        part_sums = sb.tile([P, 2], F32, name="part_sums", tag="after_part_total")
        weighted = [sb.tile([P, G // 2, RUN], F32, name=f"weighted{h}") for h in range(2)]
        for h in range(2):
            nc.scalar.activation(
                parts[h][:],
                probs[h][:],
                ACT.Ln,
                bias=1.0,
                scale=ln_scale[:, h : h + 1],
                accum_out=part_sums[:, h : h + 1],
            )
            nc.vector.tensor_tensor(
                weighted[h][:].rearrange("p g k -> p (g k)"), parts[h][:], slot_worth[h][:], ALU.mult
            )
        part_total = sb.tile([P, 1], F32, name="part_total")
        nc.scalar.activation(part_total[:], part_sums[:, 0:1], ACT.Identity, bias=part_sums[:, 1:2])
        run_sums = sb.tile([P, G], F32, name="run_sums", tag="after_part_total")
        inv_parts = sb.tile([P, 1], F32, name="inv_parts")
        norm = sb.tile([P, G], F32, name="norm")
        nc.vector.reciprocal(inv_parts[:], part_total[:])
        nc.vector.tensor_reduce(run_sums[:, 0 : G // 2], weighted[0][:], AX.X, ALU.add)
        nc.vector.tensor_scalar(norm[:], inv_parts[:].to_broadcast([P, G]), GAIN, None, ALU.mult)
        nc.vector.tensor_reduce(run_sums[:, G // 2 : G], weighted[1][:], AX.X, ALU.add)
        nc.vector.tensor_tensor(placed[:].indirect(run_list[:]), run_sums[:], norm[:], ALU.mult)

        for h, queue in enumerate((nc.sync, nc.scalar)):
            cols = slice(h * M // 2, (h + 1) * M // 2)
            result = sb.tile([P, M // 2], F32, name=f"result{h}")
            nc.vector.tensor_tensor(result[:], placed[:, cols], old_sums[:, cols], ALU.add)
            queue.dma_start(out[:, cols], result[:])
